import numpy as np
import ml_dtypes


def mxq(x, axis, fmt="e4m3"):
    dtype, down = {"e4m3": (ml_dtypes.float8_e4m3fn, 7), "e5m2": (ml_dtypes.float8_e5m2, 14)}[fmt]
    v = np.moveaxis(np.asarray(x, np.float32).astype(ml_dtypes.bfloat16).astype(np.float64), axis, -1)
    blocks = v.reshape(v.shape[:-1] + (-1, 32))
    amax = np.abs(blocks).max(-1, keepdims=True)
    byte = np.maximum(np.where(amax > 0, np.frexp(amax)[1] - 1 + 127, 0) - down, 1)
    scale = np.exp2(byte - 127.0)
    codes = (blocks / scale).astype(np.float32).astype(dtype).astype(np.float64)
    return np.moveaxis((codes * scale).reshape(v.shape), -1, axis)


WIDE = False


def mx_kscale(k):
    if not WIDE:
        return np.ones(k)
    levels = np.array([10, -10, 5, -5, 0])
    if k % 512:
        return np.exp2(np.random.permutation(np.resize(levels, k // 32))).repeat(32)
    a = np.empty((k // 512, 16))
    for p in range(k // 512):
        a[p, :8] = np.random.permutation(np.resize(levels, 8))
        for g in range(8):
            far = levels[np.abs(levels - a[p, g]) >= 10]
            a[p, g + 8] = far[np.random.randint(len(far))]
    return np.exp2(a.ravel()).repeat(32)


def f64(x):
    return np.asarray(x).astype(np.float64)


def striped(idx):
    return np.tile(idx.reshape(-1, 16).T, (8, 1)).astype(np.uint16)


def unstriped(offs):
    return offs[:16].T.reshape(-1).astype(np.int64)


def striped8(idx):
    return np.concatenate([x.reshape(-1, 16).T for x in idx]).astype(np.uint16)


def runs(offs, k):
    lists = np.stack([offs[16 * r : 16 * r + 16].T.reshape(-1) for r in range(8)]).astype(np.int64)
    return lists[np.arange(k) % 512 // 64]


def pack_weight(w):
    k, n = w.shape
    w = f64(np.asarray(w, np.float32).astype(ml_dtypes.bfloat16)).reshape(k // 32, 32, n)
    amax = np.abs(w).max(1)
    byte = np.clip(np.where(amax > 0, np.frexp(amax)[1] - 1 + 127 - 7, 1), 1, 254)
    scaled = (w * np.exp2(127.0 - byte)[:, None, :]).reshape(k, n).astype(np.float32)
    words = np.ascontiguousarray(scaled.reshape(k // 512, 128, 4, n).transpose(0, 1, 3, 2)).astype(ml_dtypes.float8_e4m3fn).view(np.uint8)
    return words, np.ascontiguousarray(byte.astype(np.uint8).reshape(k // 512, 16, n))


def unpack_weight(words, scales):
    g, p, n, _ = words.shape
    vals = np.ascontiguousarray(words).view(ml_dtypes.float8_e4m3fn).astype(np.float64) * np.repeat(np.exp2(scales.astype(np.float64) - 127.0), 8, axis=1)[..., None]
    return vals.transpose(0, 1, 3, 2).reshape(g * 512, n)


K, T, S, N, H, W = 512, 2048, 512, 512, 512, 256


def setup_inputs():
    n = np.random.standard_normal
    s = mx_kscale(K)[:, None]
    u = mx_kscale(H)
    packed_xT = pack_weight(n((K, T)) * s)
    perm = np.stack([np.random.permutation(S) for _ in range(8)])
    return {
        "x_words": packed_xT[0],
        "x_scales": packed_xT[1],
        "w1": (n((K, H)) / np.sqrt(K) / s).astype(np.float32),
        "w2": (n((K, H)) / np.sqrt(K) / s).astype(np.float32),
        "gn": (np.random.uniform(0.5, 1.5, (H, 1)) * u[:, None]).astype(np.float32),
        "w3": (n((H, H)) / np.sqrt(H) / u[:, None]).astype(np.float32),
        "res": (1.5 * n((N, S))).astype(np.float32),
        "w4": (n((H, N)) / np.sqrt(H) / u[:, None]).astype(np.float32),
        "offs": striped(np.random.permutation(T)[:S]),
        "two": striped(np.random.permutation(T)[:S]),
        "n1": striped8(perm[:, :W]),
        "n2": striped8(perm[:, W:]),
        "n3": striped8(np.stack([np.random.permutation(S) for _ in range(8)])),
        "n4": striped8(np.stack([np.random.permutation(S) for _ in range(8)])),
    }


def reference(x_words, x_scales, w1, w2, gn, w3, res, w4, offs, two, n1, n2, n3, n4):
    xq = unpack_weight(x_words, x_scales)[:, unstriped(offs)]
    y = mxq(f64(w1), 0, "e4m3").T @ xq
    pb = y[np.arange(H)[:, None], runs(n2, H)]
    pa = y[np.arange(H)[:, None], runs(n1, H)]
    rb = pb - (0.5 * pa)
    ra = np.sqrt((pa) ** 2 + (pb) ** 2 + 0.25)
    ds = np.zeros((H, S))
    ds[np.arange(H)[:, None], runs(n1, H)] = ra
    dt = ds.copy()
    dt[np.arange(H)[:, None], runs(n2, H)] = rb
    z = f64(gn) * dt
    h = mxq(f64(w3), 0, "e4m3").T @ mxq(z, 0, "e4m3")
    x_two = unpack_weight(x_words, x_scales)[:, unstriped(two)]
    d = mxq(f64(w2), 0, "e4m3").T @ x_two
    z2 = f64(gn) * (h[np.arange(H)[:, None], runs(n3, H)] - (np.tanh(d) * (d[np.arange(H)[:, None], runs(n4, H)])))
    return f64(res) + (mxq(f64(w4), 0, "e4m3").T @ mxq(z2, 0, "e4m3"))

@@ -1,0 +1,245 @@
+from contextlib import ExitStack
+
+import concourse.mybir as mybir
+
+F32 = mybir.dt.float32
+BF16 = mybir.dt.bfloat16
+I32 = mybir.dt.int32
+U32 = mybir.dt.uint32
+U16 = mybir.dt.uint16
+U8 = mybir.dt.uint8
+FP8X4 = mybir.dt.float8_e4m3fn_x4
+ACT = mybir.ActivationFunctionType
+ALU = mybir.AluOpType
+
+P = 128
+PACK = 4
+K = 512
+T = 2048
+S = 512
+W = 256
+FLOPS = 4 * 2 * 512 * 512 * 512
+
+
+def tile_picked_midsoftbpolar_none_p_kernel(
+    tc, x_words, x_scales, w1, w2, gn, w3, res, w4, offs, two, n1, n2, n3, n4, out
+):
+    nc = tc.nc
+    with ExitStack() as ctx:
+        lists = ctx.enter_context(tc.tile_pool(name="lists", bufs=1))
+        sb = ctx.enter_context(tc.tile_pool(name="sb", bufs=1))
+        ps = ctx.enter_context(tc.psum_pool(name="ps", bufs=1))
+
+        def tile(name, shape, dtype, tag=None):
+            return sb.tile(shape, dtype, name=name, tag=tag or name, align_bytes=64)
+
+        def bank(name, shape, tag):
+            return ps.tile(shape, F32, name=name, tag=tag)
+
+        def load_list(name, src):
+            t = lists.tile(list(src.shape), U16, name=name)
+            nc.sync.dma_start(t[:], src)
+            return t
+
+        def load_rows(name, src, c0, c1):
+            t = tile(name, [P, PACK, c1 - c0], F32)
+            nc.sync.dma_start(t[:], src.rearrange("(p j) c -> p j c", j=PACK)[:, :, c0:c1])
+            return t
+
+        xs = tile("xs", [P, T], U8)
+        nc.vector.memset(xs[:].bitcast(I32), 0)
+        quarter = tile("quarter", [P, 1], F32)
+        nc.vector.memset(quarter[:], 0.25)
+
+        warm = tile("warm", [P, 1], F32)
+        nc.scalar.activation(warm[:], quarter[:], ACT.Sqrt, bias=quarter[:])
+        offs_t = load_list("offs_t", offs)
+        two_t = load_list("two_t", two)
+        w1a = load_rows("w1a", w1, 0, 256)
+        for q in range(4):
+            nc.sync.dma_start(xs[32 * q : 32 * q + 4, :].bitcast(I32), x_scales[0, 4 * q : 4 * q + 4, :].bitcast(I32))
+        w1b = load_rows("w1b", w1, 256, 512)
+        xw = tile("xw", [P, T], U32)
+        nc.sync.dma_start(xw[:].bitcast(I32), x_words[0].rearrange("p n t -> p (n t)").bitcast(I32))
+        n1_t = load_list("n1_t", n1)
+        n2_t = load_list("n2_t", n2)
+        g = tile("g", [P, PACK], F32)
+        nc.sync.dma_start(g[:], gn.rearrange("(p t) o -> p (t o)", t=PACK))
+        w2r = load_rows("w2r", w2, 0, 512)
+        w3r = load_rows("w3r", w3, 0, 512)
+        n4_t = load_list("n4_t", n4)
+        n3_t = load_list("n3_t", n3)
+        w4r = load_rows("w4r", w4, 0, 512)
+        res_t = load_rows("res_t", res, 0, 512)
+
+        def cast(dst, raw, m0, m1, moff, copy=nc.scalar.copy):
+            copy(
+                dst[:].rearrange("p (t m j) -> p m j t", t=PACK, j=PACK)[:, m0:m1],
+                raw[:].rearrange("p j (m t) -> p m j t", t=PACK)[:, m0 - moff : m1 - moff],
+            )
+
+        def quantize(name, src, width, tag=None):
+            codes = tile(name + "_c", [P, width], U32, tag=tag)
+            scales = tile(name + "_s", [P, width], U8)
+            nc.vector.quantize_mx(out=codes[:].bitcast(FP8X4), scales=scales[:], in_=src)
+            return codes, scales
+
+        def mm(dst, wq, t, xq):
+            cols = slice(t * P, (t + 1) * P)
+            nc.tensor.matmul_mx(
+                out=dst, lhsT=wq[0][:, cols].bitcast(FP8X4), lhsT_scale=wq[1][:, cols],
+                rhs=xq[0][:].bitcast(FP8X4), rhs_scale=xq[1][:], start=True, stop=True,
+            )
+
+        xa_s = tile("xa_s", [P, S], U8)
+        nc.vector.tensor_copy(xa_s[:], xs[:].indirect(offs_t[:]))
+        xb_s = tile("xb_s", [P, S], U8)
+        nc.vector.tensor_copy(xb_s[:], xs[:].indirect(two_t[:]))
+        w1i = tile("w1i", [P, PACK * K], BF16)
+        cast(w1i, w1a, 0, 64, 0)
+        cast(w1i, w1b, 64, 128, 64)
+        w1q = quantize("w1q", w1i[:], K)
+        xa_c = tile("xa_c", [P, S], U32)
+        nc.vector.tensor_copy(xa_c[:], xw[:].indirect(offs_t[:]))
+        xb_c = tile("xb_c", [P, S], U32)
+        nc.vector.tensor_copy(xb_c[:], xw[:].indirect(two_t[:]))
+
+        y = []
+        for t in range(PACK):
+            acc = bank(f"y_ps{t}", [P, S], f"A{t}")
+            mm(acc[:], w1q, t, (xa_c, xa_s))
+            y_t = tile(f"y{t}", [P, S], F32)
+            nc.scalar.copy(y_t[:], acc[:])
+            y.append(y_t)
+        pair = []
+        ssum = tile("ssum", [P, PACK, W], F32)
+        w2i = tile("w2i", [P, PACK * K], BF16)
+        for t in range(PACK):
+            pr = tile(f"pair{t}", [P, 2, W], F32)
+            nc.vector.tensor_scalar(pr[:, 0, :], y[t][:].indirect(n1_t[:]), -0.5, 0.0, ALU.mult, ALU.add)
+            nc.vector.tensor_copy(pr[:, 1, :], y[t][:].indirect(n2_t[:]))
+            pair.append(pr)
+        for a in range(2):
+            sq = tile(f"sq{a}", [P, 2, 2, W], F32)
+            for b in range(2):
+                t = 2 * a + b
+                nc.scalar.activation(sq[:, b], pair[t][:], ACT.Square)
+                cast(w2i, w2r, 32 * t, 32 * (t + 1), 0)
+            nc.vector.scalar_tensor_tensor(ssum[:, 2 * a : 2 * a + 2, :], sq[:, :, 0, :], 4.0, sq[:, :, 1, :], ALU.mult, ALU.add)
+        ra = tile("ra", [P, PACK, W], F32)
+        for a in range(2):
+            nc.scalar.activation(ra[:, 2 * a : 2 * a + 2, :], ssum[:, 2 * a : 2 * a + 2, :], ACT.Sqrt, bias=quarter[:])
+
+        dt = []
+
+        def scatter(t, tag):
+            d = tile(f"dt{t}", [P, S], F32, tag=tag)
+            nc.vector.tensor_tensor(d[:].indirect(n2_t[:]), pair[t][:, 1, :], pair[t][:, 0, :], ALU.add)
+            nc.vector.tensor_copy(d[:].indirect(n1_t[:]), ra[:, t, :])
+            dt.append(d)
+
+        scatter(0, "sq0")
+        w2q = quantize("w2q", w2i[:], K, tag="ssum")
+        w3i = tile("w3i", [P, PACK * K], BF16)
+        for c in range(4):
+            cast(w3i, w3r, 32 * c, 32 * (c + 1), 0)
+        scatter(1, "w2i")
+        w3q = quantize("w3q", w3i[:], K)
+        scatter(2, "w3i")
+        scatter(3, "pair2")
+
+        dwin = [tile(f"dwin{t}", [P, 2 * S], F32) for t in range(PACK)]
+        for t in range(PACK):
+            acc = bank(f"d_ps{t}", [P, S], f"B{t}")
+            mm(acc[:], w2q, t, (xb_c, xb_s))
+            nc.scalar.activation(dwin[t][:, :S], acc[:], ACT.Copy, scale=g[:, t : t + 1])
+            nc.scalar.activation(dwin[(t - 1) % PACK][:, S:], acc[:], ACT.Tanh)
+        w4i = tile("w4i", [P, PACK * K], BF16, tag="ssum")
+        for c in range(4):
+            cast(w4i, w4r, 32 * c, 32 * (c + 1), 0)
+
+        zp = tile("zp", [P, 2, S, 2], BF16, tag="w4r")
+        for t in range(PACK):
+            nc.scalar.activation(zp[:, t // 2, :, t % 2], dt[t][:], ACT.Copy, scale=g[:, t : t + 1])
+        zi = tile("zi", [P, PACK * S], BF16)
+        nc.scalar.copy(
+            zi[:].bitcast(F32).rearrange("p (j u) -> p j u", u=2),
+            zp[:].rearrange("p u j e -> p u (j e)").bitcast(F32).rearrange("p u j -> p j u"),
+        )
+
+        def dgather(dst, t):
+            nc.vector.tensor_tensor(dst, dwin[t][:].indirect(n4_t[:]), dwin[(t - 1) % PACK][:, S:], ALU.mult)
+
+        u01 = tile("u01", [P, 2, S], F32)
+        dgather(u01[:, 0, :], 0)
+        dgather(u01[:, 1, :], 1)
+        zq = quantize("zq", zi[:], S)
+        w4q = quantize("w4q", w4i[:], K)
+        u32 = tile("u32", [P, 2, S], F32, tag="zi")
+        dgather(u32[:, 1, :], 2)
+        dgather(u32[:, 0, :], 3)
+        u = [u01[:, 0, :], u01[:, 1, :], u32[:, 1, :], u32[:, 0, :]]
+
+        h = []
+        for t in range(PACK):
+            acc = bank(f"h_ps{t}", [P, S], f"A{t}")
+            mm(acc[:], w3q, t, zq)
+            h_t = tile(f"h{t}", [P, S], F32)
+            nc.scalar.activation(h_t[:], acc[:], ACT.Copy, scale=g[:, t : t + 1])
+            h.append(h_t)
+
+        out_v = out.rearrange("(p t) j -> p t j", t=PACK)
+        chunks = ((0, 256), (256, 384), (384, 512))
+        first_bank = (0, 2, 3)
+        z2 = {}
+        accs = {}
+
+        def mix(c):
+            j0, j1 = chunks[c]
+            n = j1 - j0
+            if c == 1:
+                v = u32[:, :, 0:256].rearrange("p a (b j) -> p a b j", b=2)
+            else:
+                vt = tile(f"v{c}", [P, PACK, n], F32, tag="v")
+                v = vt[:].rearrange("p (a b) j -> p a b j", b=2)
+            for t in range(PACK):
+                nc.vector.tensor_tensor(
+                    v[:, t // 2, t % 2, :], h[t][:].indirect(n3_t[:, j0 // 16 : j1 // 16]), u[t][:, j0:j1], ALU.subtract
+                )
+            z2[c] = tile(f"z2_{c}", [P, PACK * n], BF16)
+            nc.scalar.copy(
+                z2[c][:].rearrange("p (c i a b) -> p c a b i", i=4, a=2, b=2),
+                v.rearrange("p a b (c i) -> p c a b i", i=4),
+            )
+
+        def product(c):
+            j0, j1 = chunks[c]
+            n = j1 - j0
+            z2q = quantize(f"z2q{c}", z2[c][:], n)
+            per = S // n
+            accs[c] = []
+            for b in range(PACK // per):
+                acc = bank(f"o_ps{c}_{b}", [P, per, n], f"B{first_bank[c] + b}")
+                for t in range(per):
+                    mm(acc[:, t, :], w4q, b * per + t, z2q)
+                accs[c].append(acc)
+
+        def finish(c):
+            j0, j1 = chunks[c]
+            n = j1 - j0
+            per = S // n
+            for b, acc in enumerate(accs[c]):
+                ts = slice(b * per, (b + 1) * per)
+                o = tile(f"o{c}_{b}", [P, per, n], F32)
+                nc.vector.tensor_tensor(o[:], acc[:], res_t[:, ts, j0:j1], ALU.add)
+                nc.sync.dma_start(out_v[:, ts, j0:j1], o[:])
+
+        mix(0)
+        mix(1)
+        product(0)
+        mix(2)
+        product(1)
+        product(2)
+        finish(0)
+        finish(1)
+        finish(2)

@@ -1,6 +1,7 @@
 from contextlib import ExitStack
 
 import concourse.mybir as mybir
+from concourse.masks import make_identity
 
 F32 = mybir.dt.float32
 BF16 = mybir.dt.bfloat16
@@ -51,6 +52,8 @@ def tile_picked_midsoftbpolar_none_p_kernel(
         quarter = tile("quarter", [P, 1], F32)
         nc.vector.memset(quarter[:], 0.25)
 
+        ident = tile("ident", [P, P], F32)
+        make_identity(nc, ident[:])
         warm = tile("warm", [P, 1], F32)
         nc.scalar.activation(warm[:], quarter[:], ACT.Sqrt, bias=quarter[:])
         offs_t = load_list("offs_t", offs)
@@ -112,41 +115,56 @@ def tile_picked_midsoftbpolar_none_p_kernel(
             nc.scalar.copy(y_t[:], acc[:])
             y.append(y_t)
         pair = []
-        ssum = tile("ssum", [P, PACK, W], F32)
         w2i = tile("w2i", [P, PACK * K], BF16)
         for t in range(PACK):
             pr = tile(f"pair{t}", [P, 2, W], F32)
             nc.vector.tensor_scalar(pr[:, 0, :], y[t][:].indirect(n1_t[:]), -0.5, 0.0, ALU.mult, ALU.add)
             nc.vector.tensor_copy(pr[:, 1, :], y[t][:].indirect(n2_t[:]))
             pair.append(pr)
-        for a in range(2):
-            sq = tile(f"sq{a}", [P, 2, 2, W], F32)
-            for b in range(2):
-                t = 2 * a + b
-                nc.scalar.activation(sq[:, b], pair[t][:], ACT.Square)
-                cast(w2i, w2r, 32 * t, 32 * (t + 1), 0)
-            nc.vector.scalar_tensor_tensor(ssum[:, 2 * a : 2 * a + 2, :], sq[:, :, 0, :], 4.0, sq[:, :, 1, :], ALU.mult, ALU.add)
         ra = tile("ra", [P, PACK, W], F32)
+        sums = [bank(f"sum_ps{a}", [P, 2, W], f"B{1 - a}") for a in range(2)]
+        for t in range(PACK):
+            turned = bank(f"turned{t}", [P, 2, W], f"A{t}")
+            for e in range(2):
+                for b in range(2):
+                    cols = slice(b * P, (b + 1) * P)
+                    nc.tensor.transpose(turned[:, e, cols], pair[t][:, e, cols], ident[:])
+            sq = tile(f"sq{t}", [P, 2, W], F32)
+            nc.scalar.activation(sq[:, 0, :], turned[:, 0, :], ACT.Square, scale=2.0)
+            nc.scalar.activation(sq[:, 1, :], turned[:, 1, :], ACT.Square)
+            for b in range(2):
+                cols = slice(b * P, (b + 1) * P)
+                for e in range(2):
+                    nc.tensor.matmul(
+                        sums[t // 2][:, t % 2, cols], sq[:, e, cols], ident[:], start=(e == 0), stop=(e == 1), is_transpose=True
+                    )
+            cast(w2i, w2r, 32 * t, 32 * (t + 1), 0)
         for a in range(2):
-            nc.scalar.activation(ra[:, 2 * a : 2 * a + 2, :], ssum[:, 2 * a : 2 * a + 2, :], ACT.Sqrt, bias=quarter[:])
+            nc.scalar.activation(ra[:, 2 * a : 2 * a + 2, :], sums[a][:], ACT.Sqrt, bias=quarter[:])
 
         dt = []
 
-        def scatter(t, tag):
+        def scatter_rb(t, tag):
             d = tile(f"dt{t}", [P, S], F32, tag=tag)
             nc.vector.tensor_tensor(d[:].indirect(n2_t[:]), pair[t][:, 1, :], pair[t][:, 0, :], ALU.add)
-            nc.vector.tensor_copy(d[:].indirect(n1_t[:]), ra[:, t, :])
             dt.append(d)
 
-        scatter(0, "sq0")
-        w2q = quantize("w2q", w2i[:], K, tag="ssum")
+        def scatter_ra(t):
+            nc.vector.tensor_copy(dt[t][:].indirect(n1_t[:]), ra[:, t, :])
+
+        scatter_rb(0, "y3")
+        scatter_rb(1, "sq0")
+        w2q = quantize("w2q", w2i[:], K, tag="chain")
+        scatter_ra(0)
+        scatter_ra(1)
+        scatter_rb(2, "w2r")
+        scatter_rb(3, "w2i")
+        scatter_ra(2)
+        scatter_ra(3)
         w3i = tile("w3i", [P, PACK * K], BF16)
         for c in range(4):
             cast(w3i, w3r, 32 * c, 32 * (c + 1), 0)
-        scatter(1, "w2i")
         w3q = quantize("w3q", w3i[:], K)
-        scatter(2, "w3i")
-        scatter(3, "pair2")
 
         dwin = [tile(f"dwin{t}", [P, 2 * S], F32) for t in range(PACK)]
         for t in range(PACK):
@@ -154,11 +172,8 @@ def tile_picked_midsoftbpolar_none_p_kernel(
             mm(acc[:], w2q, t, (xb_c, xb_s))
             nc.scalar.activation(dwin[t][:, :S], acc[:], ACT.Copy, scale=g[:, t : t + 1])
             nc.scalar.activation(dwin[(t - 1) % PACK][:, S:], acc[:], ACT.Tanh)
-        w4i = tile("w4i", [P, PACK * K], BF16, tag="ssum")
-        for c in range(4):
-            cast(w4i, w4r, 32 * c, 32 * (c + 1), 0)
 
-        zp = tile("zp", [P, 2, S, 2], BF16, tag="w4r")
+        zp = tile("zp", [P, 2, S, 2], BF16, tag="chain")
         for t in range(PACK):
             nc.scalar.activation(zp[:, t // 2, :, t % 2], dt[t][:], ACT.Copy, scale=g[:, t : t + 1])
         zi = tile("zi", [P, PACK * S], BF16)
@@ -174,7 +189,6 @@ def tile_picked_midsoftbpolar_none_p_kernel(
         dgather(u01[:, 0, :], 0)
         dgather(u01[:, 1, :], 1)
         zq = quantize("zq", zi[:], S)
-        w4q = quantize("w4q", w4i[:], K)
         u32 = tile("u32", [P, 2, S], F32, tag="zi")
         dgather(u32[:, 1, :], 2)
         dgather(u32[:, 0, :], 3)
@@ -187,6 +201,10 @@ def tile_picked_midsoftbpolar_none_p_kernel(
             h_t = tile(f"h{t}", [P, S], F32)
             nc.scalar.activation(h_t[:], acc[:], ACT.Copy, scale=g[:, t : t + 1])
             h.append(h_t)
+
+        w4i = tile("w4i", [P, PACK * K], BF16, tag="chain")
+        for c in range(4):
+            cast(w4i, w4r, 32 * c, 32 * (c + 1), 0)
 
         out_v = out.rearrange("(p t) j -> p t j", t=PACK)
         chunks = ((0, 256), (256, 384), (384, 512))
@@ -236,6 +254,7 @@ def tile_picked_midsoftbpolar_none_p_kernel(
 
         mix(0)
         mix(1)
+        w4q = quantize("w4q", w4i[:], K)
         product(0)
         mix(2)
         product(1)

@@ -29,10 +29,14 @@ def tile_picked_midsoftbpolar_none_p_kernel(
     with ExitStack() as ctx:
         lists = ctx.enter_context(tc.tile_pool(name="lists", bufs=1))
         sb = ctx.enter_context(tc.tile_pool(name="sb", bufs=1))
+        shared = ctx.enter_context(tc.tile_pool(name="shared", bufs=1))
         ps = ctx.enter_context(tc.psum_pool(name="ps", bufs=1))
 
         def tile(name, shape, dtype, tag=None):
             return sb.tile(shape, dtype, name=name, tag=tag or name, align_bytes=64)
+
+        def placed(name, shape, dtype, kib):
+            return shared.tile(shape, dtype, name=name, align_bytes=64, offset=1024 * kib)
 
         def bank(name, shape, tag):
             return ps.tile(shape, F32, name=name, tag=tag)
@@ -81,8 +85,8 @@ def tile_picked_midsoftbpolar_none_p_kernel(
                 raw[:].rearrange("p j (m t) -> p m j t", t=PACK)[:, m0 - moff : m1 - moff],
             )
 
-        def quantize(name, src, width, tag=None):
-            codes = tile(name + "_c", [P, width], U32, tag=tag)
+        def quantize(name, src, width, kib=None):
+            codes = tile(name + "_c", [P, width], U32) if kib is None else placed(name + "_c", [P, width], U32, kib)
             scales = tile(name + "_s", [P, width], U8)
             nc.vector.quantize_mx(out=codes[:].bitcast(FP8X4), scales=scales[:], in_=src)
             return codes, scales
@@ -152,9 +156,9 @@ def tile_picked_midsoftbpolar_none_p_kernel(
         def scatter_ra(t):
             nc.vector.tensor_copy(dt[t][:].indirect(n1_t[:]), ra[:, t, :])
 
-        scatter_rb(0, "y3")
-        scatter_rb(1, "sq0")
-        w2q = quantize("w2q", w2i[:], K, tag="chain")
+        scatter_rb(0, "sq0")
+        scatter_rb(1, "sq1")
+        w2q = quantize("w2q", w2i[:], K, 2)
         scatter_ra(0)
         scatter_ra(1)
         scatter_rb(2, "w2r")
@@ -173,7 +177,7 @@ def tile_picked_midsoftbpolar_none_p_kernel(
             nc.scalar.activation(dwin[t][:, :S], acc[:], ACT.Copy, scale=g[:, t : t + 1])
             nc.scalar.activation(dwin[(t - 1) % PACK][:, S:], acc[:], ACT.Tanh)
 
-        zp = tile("zp", [P, 2, S, 2], BF16, tag="chain")
+        zp = placed("zp", [P, 2, S, 2], BF16, 2)
         for t in range(PACK):
             nc.scalar.activation(zp[:, t // 2, :, t % 2], dt[t][:], ACT.Copy, scale=g[:, t : t + 1])
         zi = tile("zi", [P, PACK * S], BF16)
@@ -189,7 +193,7 @@ def tile_picked_midsoftbpolar_none_p_kernel(
         dgather(u01[:, 0, :], 0)
         dgather(u01[:, 1, :], 1)
         zq = quantize("zq", zi[:], S)
-        u32 = tile("u32", [P, 2, S], F32, tag="zi")
+        u32 = placed("u32", [P, 2, S], F32, 4)
         dgather(u32[:, 1, :], 2)
         dgather(u32[:, 0, :], 3)
         u = [u01[:, 0, :], u01[:, 1, :], u32[:, 1, :], u32[:, 0, :]]
@@ -202,13 +206,13 @@ def tile_picked_midsoftbpolar_none_p_kernel(
             nc.scalar.activation(h_t[:], acc[:], ACT.Copy, scale=g[:, t : t + 1])
             h.append(h_t)
 
-        w4i = tile("w4i", [P, PACK * K], BF16, tag="chain")
+        w4i = placed("w4i", [P, PACK * K], BF16, 0)
         for c in range(4):
             cast(w4i, w4r, 32 * c, 32 * (c + 1), 0)
 
         out_v = out.rearrange("(p t) j -> p t j", t=PACK)
         chunks = ((0, 256), (256, 384), (384, 512))
-        first_bank = (0, 2, 3)
+        out_banks = (("B0", "B1"), ("B2",), ("B3", "A0"))
         z2 = {}
         accs = {}
 
@@ -220,7 +224,7 @@ def tile_picked_midsoftbpolar_none_p_kernel(
             else:
                 vt = tile(f"v{c}", [P, PACK, n], F32, tag="v")
                 v = vt[:].rearrange("p (a b) j -> p a b j", b=2)
-            for t in range(PACK):
+            for t in (2, 3, 0, 1) if c == 1 else range(PACK):
                 nc.vector.tensor_tensor(
                     v[:, t // 2, t % 2, :], h[t][:].indirect(n3_t[:, j0 // 16 : j1 // 16]), u[t][:, j0:j1], ALU.subtract
                 )
@@ -234,10 +238,10 @@ def tile_picked_midsoftbpolar_none_p_kernel(
             j0, j1 = chunks[c]
             n = j1 - j0
             z2q = quantize(f"z2q{c}", z2[c][:], n)
-            per = S // n
+            per = PACK // len(out_banks[c])
             accs[c] = []
-            for b in range(PACK // per):
-                acc = bank(f"o_ps{c}_{b}", [P, per, n], f"B{first_bank[c] + b}")
+            for b, tag in enumerate(out_banks[c]):
+                acc = bank(f"o_ps{c}_{b}", [P, per, n], tag)
                 for t in range(per):
                     mm(acc[:, t, :], w4q, b * per + t, z2q)
                 accs[c].append(acc)
@@ -245,7 +249,7 @@ def tile_picked_midsoftbpolar_none_p_kernel(
         def finish(c):
             j0, j1 = chunks[c]
             n = j1 - j0
-            per = S // n
+            per = PACK // len(out_banks[c])
             for b, acc in enumerate(accs[c]):
                 ts = slice(b * per, (b + 1) * per)
                 o = tile(f"o{c}_{b}", [P, per, n], F32)

@@ -167,7 +167,7 @@ def tile_picked_midsoftbpolar_none_p_kernel(
         scatter_ra(3)
         w3i = tile("w3i", [P, PACK * K], BF16)
         for c in range(4):
-            cast(w3i, w3r, 32 * c, 32 * (c + 1), 0)
+            cast(w3i, w3r, 32 * c, 32 * (c + 1), 0, lambda o, i: nc.gpsimd.tensor_scalar(o, i, 1.0, 0.0, ALU.mult, ALU.add))
         w3q = quantize("w3q", w3i[:], K)
 
         dwin = [tile(f"dwin{t}", [P, 2 * S], F32) for t in range(PACK)]

from contextlib import ExitStack

import concourse.mybir as mybir
from concourse.masks import make_identity

F32 = mybir.dt.float32
BF16 = mybir.dt.bfloat16
I32 = mybir.dt.int32
U32 = mybir.dt.uint32
U16 = mybir.dt.uint16
U8 = mybir.dt.uint8
FP8X4 = mybir.dt.float8_e4m3fn_x4
ACT = mybir.ActivationFunctionType
ALU = mybir.AluOpType

P = 128
PACK = 4
K = 512
T = 2048
S = 512
W = 256
FLOPS = 4 * 2 * 512 * 512 * 512


def tile_picked_midsoftbpolar_none_p_kernel(
    tc, x_words, x_scales, w1, w2, gn, w3, res, w4, offs, two, n1, n2, n3, n4, out
):
    nc = tc.nc
    with ExitStack() as ctx:
        lists = ctx.enter_context(tc.tile_pool(name="lists", bufs=1))
        sb = ctx.enter_context(tc.tile_pool(name="sb", bufs=1))
        shared = ctx.enter_context(tc.tile_pool(name="shared", bufs=1))
        ps = ctx.enter_context(tc.psum_pool(name="ps", bufs=1))

        def tile(name, shape, dtype, tag=None):
            return sb.tile(shape, dtype, name=name, tag=tag or name, align_bytes=64)

        def placed(name, shape, dtype, kib):
            return shared.tile(shape, dtype, name=name, align_bytes=64, offset=1024 * kib)

        def bank(name, shape, tag):
            return ps.tile(shape, F32, name=name, tag=tag)

        def load_list(name, src):
            t = lists.tile(list(src.shape), U16, name=name)
            nc.sync.dma_start(t[:], src)
            return t

        def load_rows(name, src, c0, c1):
            t = tile(name, [P, PACK, c1 - c0], F32)
            nc.sync.dma_start(t[:], src.rearrange("(p j) c -> p j c", j=PACK)[:, :, c0:c1])
            return t

        xs = tile("xs", [P, T], U8)
        nc.vector.memset(xs[:].bitcast(I32), 0)
        quarter = tile("quarter", [P, 1], F32)
        nc.vector.memset(quarter[:], 0.25)

        ident = tile("ident", [P, P], F32)
        make_identity(nc, ident[:])
        warm = tile("warm", [P, 1], F32)
        nc.scalar.activation(warm[:], quarter[:], ACT.Sqrt, bias=quarter[:])
        offs_t = load_list("offs_t", offs)
        two_t = load_list("two_t", two)
        w1a = load_rows("w1a", w1, 0, 256)
        for q in range(4):
            nc.sync.dma_start(xs[32 * q : 32 * q + 4, :].bitcast(I32), x_scales[0, 4 * q : 4 * q + 4, :].bitcast(I32))
        w1b = load_rows("w1b", w1, 256, 512)
        xw = tile("xw", [P, T], U32)
        nc.sync.dma_start(xw[:].bitcast(I32), x_words[0].rearrange("p n t -> p (n t)").bitcast(I32))
        n1_t = load_list("n1_t", n1)
        n2_t = load_list("n2_t", n2)
        g = tile("g", [P, PACK], F32)
        nc.sync.dma_start(g[:], gn.rearrange("(p t) o -> p (t o)", t=PACK))
        w2r = load_rows("w2r", w2, 0, 512)
        w3r = load_rows("w3r", w3, 0, 512)
        n4_t = load_list("n4_t", n4)
        n3_t = load_list("n3_t", n3)
        w4r = load_rows("w4r", w4, 0, 512)
        res_t = load_rows("res_t", res, 0, 512)

        def cast(dst, raw, m0, m1, moff, copy=nc.scalar.copy):
            copy(
                dst[:].rearrange("p (t m j) -> p m j t", t=PACK, j=PACK)[:, m0:m1],
                raw[:].rearrange("p j (m t) -> p m j t", t=PACK)[:, m0 - moff : m1 - moff],
            )

        def quantize(name, src, width, kib=None):
            codes = tile(name + "_c", [P, width], U32) if kib is None else placed(name + "_c", [P, width], U32, kib)
            scales = tile(name + "_s", [P, width], U8)
            nc.vector.quantize_mx(out=codes[:].bitcast(FP8X4), scales=scales[:], in_=src)
            return codes, scales

        def mm(dst, wq, t, xq):
            cols = slice(t * P, (t + 1) * P)
            nc.tensor.matmul_mx(
                out=dst, lhsT=wq[0][:, cols].bitcast(FP8X4), lhsT_scale=wq[1][:, cols],
                rhs=xq[0][:].bitcast(FP8X4), rhs_scale=xq[1][:], start=True, stop=True,
            )

        xa_s = tile("xa_s", [P, S], U8)
        nc.vector.tensor_copy(xa_s[:], xs[:].indirect(offs_t[:]))
        xb_s = tile("xb_s", [P, S], U8)
        nc.vector.tensor_copy(xb_s[:], xs[:].indirect(two_t[:]))
        w1i = tile("w1i", [P, PACK * K], BF16)
        cast(w1i, w1a, 0, 64, 0)
        cast(w1i, w1b, 64, 128, 64)
        w1q = quantize("w1q", w1i[:], K)
        xa_c = tile("xa_c", [P, S], U32)
        nc.vector.tensor_copy(xa_c[:], xw[:].indirect(offs_t[:]))
        xb_c = tile("xb_c", [P, S], U32)
        nc.vector.tensor_copy(xb_c[:], xw[:].indirect(two_t[:]))

        y = []
        for t in range(PACK):
            acc = bank(f"y_ps{t}", [P, S], f"A{t}")
            mm(acc[:], w1q, t, (xa_c, xa_s))
            y_t = tile(f"y{t}", [P, S], F32)
            nc.scalar.copy(y_t[:], acc[:])
            y.append(y_t)
        pair = []
        w2i = tile("w2i", [P, PACK * K], BF16)
        for t in range(PACK):
            pr = tile(f"pair{t}", [P, 2, W], F32)
            nc.vector.tensor_scalar(pr[:, 0, :], y[t][:].indirect(n1_t[:]), -0.5, 0.0, ALU.mult, ALU.add)
            nc.vector.tensor_copy(pr[:, 1, :], y[t][:].indirect(n2_t[:]))
            pair.append(pr)
        ra = tile("ra", [P, PACK, W], F32)
        sums = [bank(f"sum_ps{a}", [P, 2, W], f"B{1 - a}") for a in range(2)]
        for t in range(PACK):
            turned = bank(f"turned{t}", [P, 2, W], f"A{t}")
            for e in range(2):
                for b in range(2):
                    cols = slice(b * P, (b + 1) * P)
                    nc.tensor.transpose(turned[:, e, cols], pair[t][:, e, cols], ident[:])
            sq = tile(f"sq{t}", [P, 2, W], F32)
            nc.scalar.activation(sq[:, 0, :], turned[:, 0, :], ACT.Square, scale=2.0)
            nc.scalar.activation(sq[:, 1, :], turned[:, 1, :], ACT.Square)
            for b in range(2):
                cols = slice(b * P, (b + 1) * P)
                for e in range(2):
                    nc.tensor.matmul(
                        sums[t // 2][:, t % 2, cols], sq[:, e, cols], ident[:], start=(e == 0), stop=(e == 1), is_transpose=True
                    )
            cast(w2i, w2r, 32 * t, 32 * (t + 1), 0)
        for a in range(2):
            nc.scalar.activation(ra[:, 2 * a : 2 * a + 2, :], sums[a][:], ACT.Sqrt, bias=quarter[:])

        dt = []

        def scatter_rb(t, tag):
            d = tile(f"dt{t}", [P, S], F32, tag=tag)
            nc.vector.tensor_tensor(d[:].indirect(n2_t[:]), pair[t][:, 1, :], pair[t][:, 0, :], ALU.add)
            dt.append(d)

        def scatter_ra(t):
            nc.vector.tensor_copy(dt[t][:].indirect(n1_t[:]), ra[:, t, :])

        scatter_rb(0, "sq0")
        scatter_rb(1, "sq1")
        w2q = quantize("w2q", w2i[:], K, 2)
        scatter_ra(0)
        scatter_ra(1)
        scatter_rb(2, "w2r")
        scatter_rb(3, "w2i")
        scatter_ra(2)
        scatter_ra(3)
        w3i = tile("w3i", [P, PACK * K], BF16)
        for c in range(4):
            cast(w3i, w3r, 32 * c, 32 * (c + 1), 0, lambda o, i: nc.gpsimd.tensor_scalar(o, i, 1.0, 0.0, ALU.mult, ALU.add))
        w3q = quantize("w3q", w3i[:], K)

        dwin = [tile(f"dwin{t}", [P, 2 * S], F32) for t in range(PACK)]
        for t in range(PACK):
            acc = bank(f"d_ps{t}", [P, S], f"B{t}")
            mm(acc[:], w2q, t, (xb_c, xb_s))
            nc.scalar.activation(dwin[t][:, :S], acc[:], ACT.Copy, scale=g[:, t : t + 1])
            nc.scalar.activation(dwin[(t - 1) % PACK][:, S:], acc[:], ACT.Tanh)

        zp = placed("zp", [P, 2, S, 2], BF16, 2)
        for t in range(PACK):
            nc.scalar.activation(zp[:, t // 2, :, t % 2], dt[t][:], ACT.Copy, scale=g[:, t : t + 1])
        zi = tile("zi", [P, PACK * S], BF16)
        nc.scalar.copy(
            zi[:].bitcast(F32).rearrange("p (j u) -> p j u", u=2),
            zp[:].rearrange("p u j e -> p u (j e)").bitcast(F32).rearrange("p u j -> p j u"),
        )

        def dgather(dst, t):
            nc.vector.tensor_tensor(dst, dwin[t][:].indirect(n4_t[:]), dwin[(t - 1) % PACK][:, S:], ALU.mult)

        u01 = tile("u01", [P, 2, S], F32)
        dgather(u01[:, 0, :], 0)
        dgather(u01[:, 1, :], 1)
        zq = quantize("zq", zi[:], S)
        u32 = placed("u32", [P, 2, S], F32, 4)
        dgather(u32[:, 1, :], 2)
        dgather(u32[:, 0, :], 3)
        u = [u01[:, 0, :], u01[:, 1, :], u32[:, 1, :], u32[:, 0, :]]

        h = []
        for t in range(PACK):
            acc = bank(f"h_ps{t}", [P, S], f"A{t}")
            mm(acc[:], w3q, t, zq)
            h_t = tile(f"h{t}", [P, S], F32)
            nc.scalar.activation(h_t[:], acc[:], ACT.Copy, scale=g[:, t : t + 1])
            h.append(h_t)

        w4i = placed("w4i", [P, PACK * K], BF16, 0)
        for c in range(4):
            cast(w4i, w4r, 32 * c, 32 * (c + 1), 0)

        out_v = out.rearrange("(p t) j -> p t j", t=PACK)
        chunks = ((0, 256), (256, 384), (384, 512))
        out_banks = (("B0", "B1"), ("B2",), ("B3", "A0"))
        z2 = {}
        accs = {}

        def mix(c):
            j0, j1 = chunks[c]
            n = j1 - j0
            if c == 1:
                v = u32[:, :, 0:256].rearrange("p a (b j) -> p a b j", b=2)
            else:
                vt = tile(f"v{c}", [P, PACK, n], F32, tag="v")
                v = vt[:].rearrange("p (a b) j -> p a b j", b=2)
            for t in (2, 3, 0, 1) if c == 1 else range(PACK):
                nc.vector.tensor_tensor(
                    v[:, t // 2, t % 2, :], h[t][:].indirect(n3_t[:, j0 // 16 : j1 // 16]), u[t][:, j0:j1], ALU.subtract
                )
            z2[c] = tile(f"z2_{c}", [P, PACK * n], BF16)
            nc.scalar.copy(
                z2[c][:].rearrange("p (c i a b) -> p c a b i", i=4, a=2, b=2),
                v.rearrange("p a b (c i) -> p c a b i", i=4),
            )

        def product(c):
            j0, j1 = chunks[c]
            n = j1 - j0
            z2q = quantize(f"z2q{c}", z2[c][:], n)
            per = PACK // len(out_banks[c])
            accs[c] = []
            for b, tag in enumerate(out_banks[c]):
                acc = bank(f"o_ps{c}_{b}", [P, per, n], tag)
                for t in range(per):
                    mm(acc[:, t, :], w4q, b * per + t, z2q)
                accs[c].append(acc)

        def finish(c):
            j0, j1 = chunks[c]
            n = j1 - j0
            per = PACK // len(out_banks[c])
            for b, acc in enumerate(accs[c]):
                ts = slice(b * per, (b + 1) * per)
                o = tile(f"o{c}_{b}", [P, per, n], F32)
                nc.vector.tensor_tensor(o[:], acc[:], res_t[:, ts, j0:j1], ALU.add)
                nc.sync.dma_start(out_v[:, ts, j0:j1], o[:])

        mix(0)
        mix(1)
        w4q = quantize("w4q", w4i[:], K)
        product(0)
        mix(2)
        product(1)
        product(2)
        finish(0)
        finish(1)
        finish(2)
